import numpy as np
import ml_dtypes


def mxq(x, axis, fmt="e4m3"):
    dtype, down = {"e4m3": (ml_dtypes.float8_e4m3fn, 7), "e5m2": (ml_dtypes.float8_e5m2, 14)}[fmt]
    v = np.moveaxis(np.asarray(x, np.float32).astype(ml_dtypes.bfloat16).astype(np.float64), axis, -1)
    blocks = v.reshape(v.shape[:-1] + (-1, 32))
    amax = np.abs(blocks).max(-1, keepdims=True)
    byte = np.maximum(np.where(amax > 0, np.frexp(amax)[1] - 1 + 127, 0) - down, 1)
    scale = np.exp2(byte - 127.0)
    codes = (blocks / scale).astype(np.float32).astype(dtype).astype(np.float64)
    return np.moveaxis((codes * scale).reshape(v.shape), -1, axis)


WIDE = False


def mx_kscale(k, group=512):
    if not WIDE:
        return np.ones(k)
    levels = np.array([18, -18])
    if group != 512:
        return np.exp2(np.random.permutation(np.resize(levels, k // group))).repeat(group)
    if k % 512:
        return np.exp2(np.random.permutation(np.resize(levels, k // 32))).repeat(32)
    a = np.empty((k // 512, 16))
    for p in range(k // 512):
        a[p, :8] = np.random.permutation(np.resize(levels, 8))
        for g in range(8):
            far = levels[np.abs(levels - a[p, g]) >= 10]
            a[p, g + 8] = far[np.random.randint(len(far))]
    return np.exp2(a.ravel()).repeat(32)


def f64(x):
    return np.asarray(x).astype(np.float64)


def bf(x):
    return np.asarray(x, np.float32).astype(ml_dtypes.bfloat16)


def planes(Y):
    r, m = Y.shape
    b = f64(bf(Y)).reshape(r // 32, 32, m)
    amax = np.abs(b).max(1)
    byte = np.clip(np.where(amax > 0, np.frexp(amax)[1] - 1 + 127 - 7, 1), 1, 254)
    codes = (b * np.exp2(127.0 - byte)[:, None, :]).reshape(r, m).astype(np.float32).astype(ml_dtypes.float8_e4m3fn).view(np.uint8)
    words = codes.reshape(r // 512, 128, 4, m).transpose(0, 1, 3, 2)
    return np.ascontiguousarray(words), np.ascontiguousarray(byte.astype(np.uint8).reshape(r // 512, 16, m))


G, D, M, N = 4, 128, 128, 512


def setup_inputs():
    n = np.random.standard_normal
    s_d = mx_kscale(D, 0)
    return {
        "x": (n((G, D, N)) * s_d[:, None]).astype(np.float32),
        "fc": (np.cos(2 * np.pi * np.outer(np.arange(D), np.arange(M)) / D) * (2 / np.sqrt(D)) / s_d[:, None]).astype(np.float32),
        "fs": (np.sin(2 * np.pi * (np.outer(np.arange(D), np.arange(M)) + 0.25) / D) * (2 / np.sqrt(D)) / s_d[:, None]).astype(np.float32),
    }


def reference(x, fc, fs):
    fcq = mxq(f64(fc), 0, "e4m3")
    xq = mxq(f64(x), 1, "e4m3")
    re = fcq.T @ xq
    fsq = mxq(f64(fs), 0, "e4m3")
    im = fsq.T @ xq
    y = 0.5 * np.log(np.square(re) + np.square(im) + 0.001)
    Y = y.reshape(G * M, N)
    words, scales = planes(Y)
    return Y, words, scales

@@ -1,0 +1,204 @@
+from contextlib import ExitStack
+
+import concourse.mybir as mybir
+
+G, D, M, N = 4, 128, 128, 512
+FLOPS = 2 * 2 * G * D * M * N
+
+F32 = mybir.dt.float32
+BF16 = mybir.dt.bfloat16
+U32 = mybir.dt.uint32
+I32 = mybir.dt.int32
+U8 = mybir.dt.uint8
+FP8X4 = mybir.dt.float8_e4m3fn_x4
+ACT = mybir.ActivationFunctionType
+ALU = mybir.AluOpType
+
+P = 128
+R = 32
+PACK = 4
+CH = 128
+EPS = 0.001
+STAGES = ((0, 1), (2,), (3,))
+
+
+def walk_src(ap):
+    return ap.rearrange("p t (c i) -> p c t i", i=4)
+
+
+def walk_dst(ap):
+    return ap.rearrange("p (c i) t -> p c t i", i=4)
+
+
+def tile_rows_pl_dft_logmag_kernel(tc, x, fc, fs, out_0, out_1, out_2):
+    nc = tc.nc
+    x_rows = x.rearrange("g d n -> (g d) n").rearrange("(q j) n -> q j n", j=PACK)
+    y_rows = out_0.rearrange("(q t) n -> q t n", t=PACK)
+    words_out = out_1.rearrange("v p n u -> (v p) (n u)").bitcast(I32)
+    scales_out = out_2.rearrange("v f n -> (v f) n").bitcast(I32)
+
+    with ExitStack() as ctx:
+        sb = ctx.enter_context(tc.tile_pool(name="sb", bufs=1))
+        ps = ctx.enter_context(tc.psum_pool(name="ps", bufs=1))
+        ctx.enter_context(tc.manual_schedule())
+
+        def new(name, shape, dtype):
+            return sb.tile(shape, dtype, name=name, align_bytes=64)
+
+        f_raw = [new("f_raw%d" % k, [P, PACK, M], F32) for k in range(2)]
+        f_bf = new("f_bf", [P, 2 * M * PACK], BF16)
+        f_q = new("f_q", [P, 2 * M + 2 * M // 4], U32)
+        f_rep = new("f_rep", [P, 2 * M + 2 * M // 4], U32)
+        x_raw = [new("x_raw%d" % h, [P, PACK, 2 * CH], F32) for h in range(2)]
+        x_bf = [new("x_bf%d" % c, [P, CH * PACK], BF16) for c in range(4)]
+        x_codes = [new("x_codes%d" % c, [P, CH], U32) for c in range(4)]
+        x_scales = [new("x_scales%d" % c, [P, CH], U8) for c in range(4)]
+        y_codes = new("y_codes", [P, N], U32)
+        y_scales = new("y_scales", [P, N], U8)
+        one = new("one", [P, 1], F32)
+        warm = new("warm", [P, 1], F32)
+        banks = {}
+        for g in range(G):
+            for h in range(2):
+                banks[(g, h)] = ps.tile([P, 2, 2, CH], F32, name="bank%d_%d" % (g, h))
+
+        for k, f in enumerate((fc, fs)):
+            for g in (0, 2):
+                nc.sync.dma_start(out=f_raw[k][R * g : R * g + R, :, :], in_=f.rearrange("(p j) m -> p j m", j=PACK))
+        for h in range(2):
+            nc.sync.dma_start(out=x_raw[h][:], in_=x_rows[:, :, 2 * CH * h : 2 * CH * (h + 1)])
+
+        nc.vector.memset(one[:], 1.0)
+        nc.scalar.activation(out=warm[:], in_=one[:], func=ACT.Ln)
+        for k in range(2):
+            for g in (1, 3):
+                nc.vector.memset(f_raw[k][R * g : R * g + R, :, :], 0.0)
+        nc.vector.memset(f_q[:, 2 * M :], 0)
+
+        def f_bf_view(k):
+            return f_bf[:, k * M * PACK : (k + 1) * M * PACK].rearrange("p (m t) -> p m t", t=PACK)
+
+        nc.vector.tensor_copy(out=walk_dst(f_bf_view(0)), in_=walk_src(f_raw[0][:]))
+        nc.scalar.copy(out=walk_dst(f_bf_view(1)), in_=walk_src(f_raw[1][:]))
+        nc.vector.quantize_mx(out=f_q[:, : 2 * M].bitcast(FP8X4), scales=f_q[:, 2 * M :].bitcast(U8), in_=f_bf[:])
+        for g in (0, 2):
+            nc.sync.dma_start(
+                out=f_rep[R * (g + 1) : R * (g + 2), :].bitcast(I32), in_=f_q[R * g : R * (g + 1), :].bitcast(I32)
+            )
+
+        def round_x(c, copy):
+            src = x_raw[c // 2][:, :, (c % 2) * CH : (c % 2 + 1) * CH]
+            copy(out=walk_dst(x_bf[c][:].rearrange("p (n t) -> p n t", t=PACK)), in_=walk_src(src))
+
+        def quant_x(c):
+            nc.vector.quantize_mx(out=x_codes[c][:].bitcast(FP8X4), scales=x_scales[c][:], in_=x_bf[c][:])
+
+        def products(groups, h):
+            for c in (2 * h, 2 * h + 1):
+                for k in range(2):
+                    for g in groups:
+                        rows = slice(R * g, R * g + R)
+                        f_tile = f_q if g % 2 == 0 else f_rep
+                        nc.tensor.matmul_mx(
+                            out=banks[(g, h)][:, c % 2, k, :],
+                            lhsT=f_tile[rows, k * M : (k + 1) * M].bitcast(FP8X4),
+                            lhsT_scale=f_tile[rows, 2 * M :].bitcast(U8)[:, k * M : (k + 1) * M],
+                            rhs=x_codes[c][rows, :].bitcast(FP8X4),
+                            rhs_scale=x_scales[c][rows, :],
+                            start=True,
+                            stop=True,
+                        )
+
+        power = [new("power%d" % s, [P, PACK, CH * len(cs)], F32) for s, cs in enumerate(STAGES)]
+
+        def square(g, s):
+            cs = STAGES[s]
+            w = len(cs)
+            lo = cs[0] % 2
+            sq = new("sq%d_%d" % (g, s), [P, w, 2, CH], F32)
+            nc.scalar.activation(out=sq[:], in_=banks[(g, cs[0] // 2)][:, lo : lo + w, :, :], func=ACT.Square)
+            tot = new("tot%d_%d" % (g, s), [P, w, CH], F32)
+            nc.vector.scalar_tensor_tensor(
+                out=tot[:], in0=sq[:, :, 0, :], scalar=EPS, in1=sq[:, :, 1, :], op0=ALU.add, op1=ALU.add
+            )
+            nc.sync.dma_start(out=power[s][R * g : R * g + R, :, :], in_=tot[:].rearrange("p c n -> p (c n)"))
+
+        round_x(0, nc.vector.tensor_copy)
+        round_x(1, nc.scalar.copy)
+        quant_x(0)
+        quant_x(1)
+        products((0, 2), 0)
+        products((1, 3), 0)
+        round_x(2, nc.vector.tensor_copy)
+        round_x(3, nc.vector.tensor_copy)
+        quant_x(2)
+        quant_x(3)
+        products((0, 2, 1, 3), 1)
+        for s in range(len(STAGES)):
+            for g in (0, 2, 1, 3):
+                square(g, s)
+
+        logs = [new("logs%d" % c, [P, PACK, CH], F32) for c in range(4)]
+        y_bf = [new("y_bf%d" % c, [P, CH * PACK], BF16) for c in range(4)]
+        y = [new("y%d" % s, [P, PACK, CH * len(cs)], F32) for s, cs in enumerate(STAGES)]
+        place = {}
+        for s, cs in enumerate(STAGES):
+            for i, c in enumerate(cs):
+                place[c] = (s, slice(i * CH, (i + 1) * CH))
+
+        def log(c):
+            s, cols = place[c]
+            nc.scalar.activation(out=logs[c][:], in_=power[s][:, :, cols], func=ACT.Ln)
+
+        def halve_v(c):
+            s, cols = place[c]
+            nc.vector.tensor_scalar(out=y[s][:, :, cols], in0=logs[c][:], scalar1=0.5, scalar2=None, op0=ALU.mult)
+
+        def halve_a(c):
+            s, cols = place[c]
+            nc.scalar.activation(out=y[s][:, :, cols], in_=logs[c][:], func=ACT.Copy, scale=0.5)
+
+        def round_y(c):
+            nc.vector.tensor_scalar(
+                out=walk_dst(y_bf[c][:].rearrange("p (n t) -> p n t", t=PACK)),
+                in0=walk_src(logs[c][:]),
+                scalar1=0.5,
+                scalar2=None,
+                op0=ALU.mult,
+            )
+
+        def quant_y(c):
+            cols = slice(c * CH, (c + 1) * CH)
+            nc.vector.quantize_mx(out=y_codes[:, cols].bitcast(FP8X4), scales=y_scales[:, cols], in_=y_bf[c][:])
+
+        def store_y(s, eng):
+            cs = STAGES[s]
+            eng.dma_start(out=y_rows[:, :, cs[0] * CH : (cs[-1] + 1) * CH], in_=y[s][:])
+
+        def store_words(lo, hi, eng):
+            eng.dma_start(out=words_out[:, lo * CH : hi * CH], in_=y_codes[:, lo * CH : hi * CH].bitcast(I32))
+
+        log(0)
+        round_y(0)
+        halve_v(0)
+        quant_y(0)
+        log(1)
+        round_y(1)
+        halve_v(1)
+        quant_y(1)
+        store_y(0, nc.sync)
+        store_words(0, 2, nc.sync)
+        log(2)
+        halve_a(2)
+        store_y(1, nc.sync)
+        round_y(2)
+        log(3)
+        halve_a(3)
+        store_y(2, nc.scalar)
+        quant_y(2)
+        round_y(3)
+        quant_y(3)
+        store_words(2, 4, nc.sync)
+        for q in range(4):
+            eng = nc.sync if q % 2 == 0 else nc.scalar
+            eng.dma_start(out=scales_out[4 * q : 4 * q + 4, :], in_=y_scales[R * q : R * q + 4, :].bitcast(I32))

@@ -19,7 +19,8 @@ R = 32
 PACK = 4
 CH = 128
 EPS = 0.001
-STAGES = ((0, 1), (2,), (3,))
+LOADS = ((0, 128), (128, 256), (256, 512))
+ORDER = (0, 2, 1, 3)
 
 
 def walk_src(ap):
@@ -27,7 +28,7 @@ def walk_src(ap):
 
 
 def walk_dst(ap):
-    return ap.rearrange("p (c i) t -> p c t i", i=4)
+    return ap.rearrange("p (c i t) -> p c t i", i=4, t=PACK)
 
 
 def tile_rows_pl_dft_logmag_kernel(tc, x, fc, fs, out_0, out_1, out_2):
@@ -45,160 +46,199 @@ def tile_rows_pl_dft_logmag_kernel(tc, x, fc, fs, out_0, out_1, out_2):
         def new(name, shape, dtype):
             return sb.tile(shape, dtype, name=name, align_bytes=64)
 
-        f_raw = [new("f_raw%d" % k, [P, PACK, M], F32) for k in range(2)]
-        f_bf = new("f_bf", [P, 2 * M * PACK], BF16)
-        f_q = new("f_q", [P, 2 * M + 2 * M // 4], U32)
-        f_rep = new("f_rep", [P, 2 * M + 2 * M // 4], U32)
-        x_raw = [new("x_raw%d" % h, [P, PACK, 2 * CH], F32) for h in range(2)]
-        x_bf = [new("x_bf%d" % c, [P, CH * PACK], BF16) for c in range(4)]
-        x_codes = [new("x_codes%d" % c, [P, CH], U32) for c in range(4)]
-        x_scales = [new("x_scales%d" % c, [P, CH], U8) for c in range(4)]
+        f_raw = new("f_raw", [P, PACK, M], F32)
+        f_bf = new("f_bf", [P, M * PACK], BF16)
+        f_q = [new("f_q%d" % k, [P, M + M // 4], U32) for k in range(2)]
+        x_raw = [new("x_raw%d" % i, [P, PACK, hi - lo], F32) for i, (lo, hi) in enumerate(LOADS)]
+        x_bf = new("x_bf", [P, N * PACK], BF16)
+        x_codes = new("x_codes", [P, N], U32)
+        x_scales = new("x_scales", [P, N], U8)
+        sq = [new("sq%d" % g, [P, 2, N], F32) for g in range(G)]
+        kept = [new("kept%d" % g, [P, 2, N], F32) for g in range(G)]
+        tot = [new("tot%d" % g, [P, N], F32) for g in range(G)]
+        power = new("power", [P, PACK, N], F32)
+        logs = new("logs", [P, PACK, N], F32)
+        y = new("y", [P, PACK, N], F32)
+        y_bf = new("y_bf", [P, N * PACK], BF16)
         y_codes = new("y_codes", [P, N], U32)
         y_scales = new("y_scales", [P, N], U8)
         one = new("one", [P, 1], F32)
         warm = new("warm", [P, 1], F32)
-        banks = {}
-        for g in range(G):
-            for h in range(2):
-                banks[(g, h)] = ps.tile([P, 2, 2, CH], F32, name="bank%d_%d" % (g, h))
+        banks = [[ps.tile([P, 4 * CH], F32, name="bank%d_%d" % (g, h)) for h in range(2)] for g in range(G)]
 
-        for k, f in enumerate((fc, fs)):
-            for g in (0, 2):
-                nc.sync.dma_start(out=f_raw[k][R * g : R * g + R, :, :], in_=f.rearrange("(p j) m -> p j m", j=PACK))
-        for h in range(2):
-            nc.sync.dma_start(out=x_raw[h][:], in_=x_rows[:, :, 2 * CH * h : 2 * CH * (h + 1)])
+        def load_f():
+            for g in ORDER:
+                f = fc if g < 2 else fs
+                nc.sync.dma_start(out=f_raw[R * g : R * g + R, :, :], in_=f.rearrange("(p j) m -> p j m", j=PACK))
 
-        nc.vector.memset(one[:], 1.0)
-        nc.scalar.activation(out=warm[:], in_=one[:], func=ACT.Ln)
-        for k in range(2):
-            for g in (1, 3):
-                nc.vector.memset(f_raw[k][R * g : R * g + R, :, :], 0.0)
-        nc.vector.memset(f_q[:, 2 * M :], 0)
+        def load_x(i):
+            lo, hi = LOADS[i]
+            nc.sync.dma_start(out=x_raw[i][:], in_=x_rows[:, :, lo:hi])
 
-        def f_bf_view(k):
-            return f_bf[:, k * M * PACK : (k + 1) * M * PACK].rearrange("p (m t) -> p m t", t=PACK)
+        def round_f(copy):
+            copy(out=walk_dst(f_bf[:]), in_=walk_src(f_raw[:]))
 
-        nc.vector.tensor_copy(out=walk_dst(f_bf_view(0)), in_=walk_src(f_raw[0][:]))
-        nc.scalar.copy(out=walk_dst(f_bf_view(1)), in_=walk_src(f_raw[1][:]))
-        nc.vector.quantize_mx(out=f_q[:, : 2 * M].bitcast(FP8X4), scales=f_q[:, 2 * M :].bitcast(U8), in_=f_bf[:])
-        for g in (0, 2):
-            nc.sync.dma_start(
-                out=f_rep[R * (g + 1) : R * (g + 2), :].bitcast(I32), in_=f_q[R * g : R * (g + 1), :].bitcast(I32)
+        def quant_f():
+            nc.vector.quantize_mx(out=f_q[0][:, :M].bitcast(FP8X4), scales=f_q[0][:, M:].bitcast(U8), in_=f_bf[:])
+            for half in range(2):
+                nc.sync.dma_start(
+                    out=f_q[1][64 * half : 64 * half + 64, :].bitcast(I32),
+                    in_=f_q[0][64 * (1 - half) : 64 * (1 - half) + 64, :].bitcast(I32),
+                )
+
+        def round_x(lo, hi, copy):
+            for i, (a, b) in enumerate(LOADS):
+                if a <= lo and hi <= b:
+                    copy(out=walk_dst(x_bf[:, PACK * lo : PACK * hi]), in_=walk_src(x_raw[i][:, :, lo - a : hi - a]))
+
+        def quant_x(lo, hi):
+            nc.vector.quantize_mx(
+                out=x_codes[:, lo:hi].bitcast(FP8X4), scales=x_scales[:, lo:hi], in_=x_bf[:, PACK * lo : PACK * hi]
             )
 
-        def round_x(c, copy):
-            src = x_raw[c // 2][:, :, (c % 2) * CH : (c % 2 + 1) * CH]
-            copy(out=walk_dst(x_bf[c][:].rearrange("p (n t) -> p n t", t=PACK)), in_=walk_src(src))
+        def product(g, k, c, h, slot):
+            rows = slice(R * g, R * g + R)
+            cols = slice(c * CH, (c + 1) * CH)
+            nc.tensor.matmul_mx(
+                out=banks[g][h][:, slot * CH : (slot + 1) * CH],
+                lhsT=f_q[k][rows, :M].bitcast(FP8X4),
+                lhsT_scale=f_q[k][rows, M:].bitcast(U8),
+                rhs=x_codes[rows, cols].bitcast(FP8X4),
+                rhs_scale=x_scales[rows, cols],
+                start=True,
+                stop=True,
+            )
 
-        def quant_x(c):
-            nc.vector.quantize_mx(out=x_codes[c][:].bitcast(FP8X4), scales=x_scales[c][:], in_=x_bf[c][:])
+        def views(g, k, lo, hi, h, at):
+            if k is None:
+                src = banks[g][h][:, at : at + 2 * CH].rearrange("p (k n) -> p k n", k=2)[:, :, lo % CH : lo % CH + hi - lo]
+                return src, (lambda t: t[g][:, :, lo:hi])
+            return banks[g][h][:, at : at + hi - lo], (lambda t: t[g][:, k, lo:hi])
 
-        def products(groups, h):
-            for c in (2 * h, 2 * h + 1):
-                for k in range(2):
-                    for g in groups:
-                        rows = slice(R * g, R * g + R)
-                        f_tile = f_q if g % 2 == 0 else f_rep
-                        nc.tensor.matmul_mx(
-                            out=banks[(g, h)][:, c % 2, k, :],
-                            lhsT=f_tile[rows, k * M : (k + 1) * M].bitcast(FP8X4),
-                            lhsT_scale=f_tile[rows, 2 * M :].bitcast(U8)[:, k * M : (k + 1) * M],
-                            rhs=x_codes[c][rows, :].bitcast(FP8X4),
-                            rhs_scale=x_scales[c][rows, :],
-                            start=True,
-                            stop=True,
-                        )
+        def square(g, k, lo, hi, h, at):
+            src, pick = views(g, k, lo, hi, h, at)
+            nc.scalar.activation(out=pick(sq), in_=src, func=ACT.Square)
 
-        power = [new("power%d" % s, [P, PACK, CH * len(cs)], F32) for s, cs in enumerate(STAGES)]
+        def keep(g, k, lo, hi, h, at):
+            src, pick = views(g, k, lo, hi, h, at)
+            nc.vector.tensor_copy(out=pick(kept), in_=src)
 
-        def square(g, s):
-            cs = STAGES[s]
-            w = len(cs)
-            lo = cs[0] % 2
-            sq = new("sq%d_%d" % (g, s), [P, w, 2, CH], F32)
-            nc.scalar.activation(out=sq[:], in_=banks[(g, cs[0] // 2)][:, lo : lo + w, :, :], func=ACT.Square)
-            tot = new("tot%d_%d" % (g, s), [P, w, CH], F32)
+        def times(g, k, lo, hi, h, at):
+            src, pick = views(g, k, lo, hi, h, at)
+            nc.vector.tensor_tensor(out=pick(sq), in0=src, in1=pick(kept), op=ALU.mult)
+
+        def add(g, lo, hi):
             nc.vector.scalar_tensor_tensor(
-                out=tot[:], in0=sq[:, :, 0, :], scalar=EPS, in1=sq[:, :, 1, :], op0=ALU.add, op1=ALU.add
+                out=tot[g][:, lo:hi], in0=sq[g][:, 0, lo:hi], scalar=EPS, in1=sq[g][:, 1, lo:hi], op0=ALU.add, op1=ALU.add
             )
-            nc.sync.dma_start(out=power[s][R * g : R * g + R, :, :], in_=tot[:].rearrange("p c n -> p (c n)"))
 
-        round_x(0, nc.vector.tensor_copy)
-        round_x(1, nc.scalar.copy)
-        quant_x(0)
-        quant_x(1)
-        products((0, 2), 0)
-        products((1, 3), 0)
-        round_x(2, nc.vector.tensor_copy)
-        round_x(3, nc.vector.tensor_copy)
-        quant_x(2)
-        quant_x(3)
-        products((0, 2, 1, 3), 1)
-        for s in range(len(STAGES)):
-            for g in (0, 2, 1, 3):
-                square(g, s)
+        def regroup(g, lo, hi, eng=nc.sync):
+            eng.dma_start(out=power[R * g : R * g + R, :, lo:hi], in_=tot[g][:, lo:hi])
 
-        logs = [new("logs%d" % c, [P, PACK, CH], F32) for c in range(4)]
-        y_bf = [new("y_bf%d" % c, [P, CH * PACK], BF16) for c in range(4)]
-        y = [new("y%d" % s, [P, PACK, CH * len(cs)], F32) for s, cs in enumerate(STAGES)]
-        place = {}
-        for s, cs in enumerate(STAGES):
-            for i, c in enumerate(cs):
-                place[c] = (s, slice(i * CH, (i + 1) * CH))
+        def log(lo, hi):
+            nc.scalar.activation(out=logs[:, :, lo:hi], in_=power[:, :, lo:hi], func=ACT.Ln)
 
-        def log(c):
-            s, cols = place[c]
-            nc.scalar.activation(out=logs[c][:], in_=power[s][:, :, cols], func=ACT.Ln)
+        def halve_v(lo, hi):
+            nc.vector.tensor_scalar(out=y[:, :, lo:hi], in0=logs[:, :, lo:hi], scalar1=0.5, scalar2=None, op0=ALU.mult)
 
-        def halve_v(c):
-            s, cols = place[c]
-            nc.vector.tensor_scalar(out=y[s][:, :, cols], in0=logs[c][:], scalar1=0.5, scalar2=None, op0=ALU.mult)
+        def halve_a(lo, hi):
+            nc.scalar.activation(out=y[:, :, lo:hi], in_=logs[:, :, lo:hi], func=ACT.Copy, scale=0.5)
 
-        def halve_a(c):
-            s, cols = place[c]
-            nc.scalar.activation(out=y[s][:, :, cols], in_=logs[c][:], func=ACT.Copy, scale=0.5)
-
-        def round_y(c):
+        def round_y(lo, hi):
             nc.vector.tensor_scalar(
-                out=walk_dst(y_bf[c][:].rearrange("p (n t) -> p n t", t=PACK)),
-                in0=walk_src(logs[c][:]),
+                out=walk_dst(y_bf[:, PACK * lo : PACK * hi]),
+                in0=walk_src(logs[:, :, lo:hi]),
                 scalar1=0.5,
                 scalar2=None,
                 op0=ALU.mult,
             )
 
-        def quant_y(c):
-            cols = slice(c * CH, (c + 1) * CH)
-            nc.vector.quantize_mx(out=y_codes[:, cols].bitcast(FP8X4), scales=y_scales[:, cols], in_=y_bf[c][:])
+        def quant_y(lo, hi):
+            nc.vector.quantize_mx(
+                out=y_codes[:, lo:hi].bitcast(FP8X4), scales=y_scales[:, lo:hi], in_=y_bf[:, PACK * lo : PACK * hi]
+            )
 
-        def store_y(s, eng):
-            cs = STAGES[s]
-            eng.dma_start(out=y_rows[:, :, cs[0] * CH : (cs[-1] + 1) * CH], in_=y[s][:])
+        def store_y(lo, hi, eng):
+            eng.dma_start(out=y_rows[:, :, lo:hi], in_=y[:, :, lo:hi])
 
         def store_words(lo, hi, eng):
-            eng.dma_start(out=words_out[:, lo * CH : hi * CH], in_=y_codes[:, lo * CH : hi * CH].bitcast(I32))
+            eng.dma_start(out=words_out[:, lo:hi], in_=y_codes[:, lo:hi].bitcast(I32))
 
-        log(0)
-        round_y(0)
-        halve_v(0)
-        quant_y(0)
-        log(1)
-        round_y(1)
-        halve_v(1)
-        quant_y(1)
-        store_y(0, nc.sync)
-        store_words(0, 2, nc.sync)
-        log(2)
-        halve_a(2)
-        store_y(1, nc.sync)
-        round_y(2)
-        log(3)
-        halve_a(3)
-        store_y(2, nc.scalar)
-        quant_y(2)
-        round_y(3)
-        quant_y(3)
-        store_words(2, 4, nc.sync)
-        for q in range(4):
-            eng = nc.sync if q % 2 == 0 else nc.scalar
-            eng.dma_start(out=scales_out[4 * q : 4 * q + 4, :], in_=y_scales[R * q : R * q + 4, :].bitcast(I32))
+        def store_scales(engs):
+            for q in range(4):
+                engs[q].dma_start(out=scales_out[4 * q : 4 * q + 4, :], in_=y_scales[R * q : R * q + 4, :].bitcast(I32))
+
+        V, A, S = nc.vector.tensor_copy, nc.scalar.copy, nc.sync
+        Q = nc.scalar
+        load_f()
+        load_x(0)
+        load_x(1)
+        load_x(2)
+        nc.vector.memset(one[:], 1.0)
+        nc.scalar.activation(out=warm[:], in_=one[:], func=ACT.Ln)
+        nc.vector.memset(f_q[0][:, M:], 0)
+        round_f(V)
+        quant_f()
+        round_x(0, 128, V)
+        round_x(208, 256, A)
+        quant_x(0, 128)
+        round_x(128, 208, V)
+        for g in ORDER:
+            product(g, 0, 0, 0, 0)
+        quant_x(128, 256)
+        round_x(256, 512, V)
+        quant_x(256, 512)
+        for g in ORDER:
+            square(g, 0, 0, 128, 0, 0)
+        for g in ORDER:
+            product(g, 0, 1, 1, 0)
+        for g in ORDER:
+            square(g, 0, 128, 256, 1, 0)
+        for c in range(2):
+            for g in ORDER:
+                product(g, 1, c, 0, 1 + c)
+        for g in ORDER:
+            for k in range(2):
+                product(g, k, 2, 1, k)
+        for g in ORDER:
+            square(g, 1, 0, 128, 0, CH)
+            add(g, 0, 128)
+            regroup(g, 0, 128)
+        for g in ORDER:
+            square(g, 1, 128, 256, 0, 256)
+            add(g, 128, 256)
+            regroup(g, 128, 256)
+        for g in ORDER:
+            for k in range(2):
+                product(g, k, 3, 0, k)
+        for g in ORDER:
+            square(g, None, 256, 384, 1, 0)
+            add(g, 256, 384)
+            regroup(g, 256, 384)
+        for g in ORDER:
+            square(g, None, 384, 512, 0, 0)
+            add(g, 384, 512)
+            regroup(g, 384, 512)
+        log(0, 128)
+        halve_v(0, 128)
+        store_y(0, 128, S)
+        round_y(0, 128)
+        log(128, 256)
+        halve_v(128, 256)
+        store_y(128, 256, S)
+        quant_y(0, 128)
+        round_y(128, 256)
+        log(256, 384)
+        halve_v(256, 384)
+        store_y(256, 384, S)
+        quant_y(128, 256)
+        round_y(256, 384)
+        store_words(0, 256, S)
+        quant_y(256, 384)
+        log(384, 512)
+        round_y(384, 512)
+        halve_a(384, 512)
+        store_y(384, 512, Q)
+        quant_y(384, 512)
+        store_words(256, 512, S)
+        store_scales((S, Q, S, Q))

from contextlib import ExitStack

import concourse.mybir as mybir

G, D, M, N = 4, 128, 128, 512
FLOPS = 2 * 2 * G * D * M * N

F32 = mybir.dt.float32
BF16 = mybir.dt.bfloat16
U32 = mybir.dt.uint32
I32 = mybir.dt.int32
U8 = mybir.dt.uint8
FP8X4 = mybir.dt.float8_e4m3fn_x4
ACT = mybir.ActivationFunctionType
ALU = mybir.AluOpType

P = 128
R = 32
PACK = 4
CH = 128
EPS = 0.001
LOADS = ((0, 128), (128, 256), (256, 512))
ORDER = (0, 2, 1, 3)


def walk_src(ap):
    return ap.rearrange("p t (c i) -> p c t i", i=4)


def walk_dst(ap):
    return ap.rearrange("p (c i t) -> p c t i", i=4, t=PACK)


def tile_rows_pl_dft_logmag_kernel(tc, x, fc, fs, out_0, out_1, out_2):
    nc = tc.nc
    x_rows = x.rearrange("g d n -> (g d) n").rearrange("(q j) n -> q j n", j=PACK)
    y_rows = out_0.rearrange("(q t) n -> q t n", t=PACK)
    words_out = out_1.rearrange("v p n u -> (v p) (n u)").bitcast(I32)
    scales_out = out_2.rearrange("v f n -> (v f) n").bitcast(I32)

    with ExitStack() as ctx:
        sb = ctx.enter_context(tc.tile_pool(name="sb", bufs=1))
        ps = ctx.enter_context(tc.psum_pool(name="ps", bufs=1))
        ctx.enter_context(tc.manual_schedule())

        def new(name, shape, dtype):
            return sb.tile(shape, dtype, name=name, align_bytes=64)

        f_raw = new("f_raw", [P, PACK, M], F32)
        f_bf = new("f_bf", [P, M * PACK], BF16)
        f_q = [new("f_q%d" % k, [P, M + M // 4], U32) for k in range(2)]
        x_raw = [new("x_raw%d" % i, [P, PACK, hi - lo], F32) for i, (lo, hi) in enumerate(LOADS)]
        x_bf = new("x_bf", [P, N * PACK], BF16)
        x_codes = new("x_codes", [P, N], U32)
        x_scales = new("x_scales", [P, N], U8)
        sq = [new("sq%d" % g, [P, 2, N], F32) for g in range(G)]
        kept = [new("kept%d" % g, [P, 2, N], F32) for g in range(G)]
        tot = [new("tot%d" % g, [P, N], F32) for g in range(G)]
        power = new("power", [P, PACK, N], F32)
        logs = new("logs", [P, PACK, N], F32)
        y = new("y", [P, PACK, N], F32)
        y_bf = new("y_bf", [P, N * PACK], BF16)
        y_codes = new("y_codes", [P, N], U32)
        y_scales = new("y_scales", [P, N], U8)
        one = new("one", [P, 1], F32)
        warm = new("warm", [P, 1], F32)
        banks = [[ps.tile([P, 4 * CH], F32, name="bank%d_%d" % (g, h)) for h in range(2)] for g in range(G)]

        def load_f():
            for g in ORDER:
                f = fc if g < 2 else fs
                nc.sync.dma_start(out=f_raw[R * g : R * g + R, :, :], in_=f.rearrange("(p j) m -> p j m", j=PACK))

        def load_x(i):
            lo, hi = LOADS[i]
            nc.sync.dma_start(out=x_raw[i][:], in_=x_rows[:, :, lo:hi])

        def round_f(copy):
            copy(out=walk_dst(f_bf[:]), in_=walk_src(f_raw[:]))

        def quant_f():
            nc.vector.quantize_mx(out=f_q[0][:, :M].bitcast(FP8X4), scales=f_q[0][:, M:].bitcast(U8), in_=f_bf[:])
            for half in range(2):
                nc.sync.dma_start(
                    out=f_q[1][64 * half : 64 * half + 64, :].bitcast(I32),
                    in_=f_q[0][64 * (1 - half) : 64 * (1 - half) + 64, :].bitcast(I32),
                )

        def round_x(lo, hi, copy):
            for i, (a, b) in enumerate(LOADS):
                if a <= lo and hi <= b:
                    copy(out=walk_dst(x_bf[:, PACK * lo : PACK * hi]), in_=walk_src(x_raw[i][:, :, lo - a : hi - a]))

        def quant_x(lo, hi):
            nc.vector.quantize_mx(
                out=x_codes[:, lo:hi].bitcast(FP8X4), scales=x_scales[:, lo:hi], in_=x_bf[:, PACK * lo : PACK * hi]
            )

        def product(g, k, c, h, slot):
            rows = slice(R * g, R * g + R)
            cols = slice(c * CH, (c + 1) * CH)
            nc.tensor.matmul_mx(
                out=banks[g][h][:, slot * CH : (slot + 1) * CH],
                lhsT=f_q[k][rows, :M].bitcast(FP8X4),
                lhsT_scale=f_q[k][rows, M:].bitcast(U8),
                rhs=x_codes[rows, cols].bitcast(FP8X4),
                rhs_scale=x_scales[rows, cols],
                start=True,
                stop=True,
            )

        def views(g, k, lo, hi, h, at):
            if k is None:
                src = banks[g][h][:, at : at + 2 * CH].rearrange("p (k n) -> p k n", k=2)[:, :, lo % CH : lo % CH + hi - lo]
                return src, (lambda t: t[g][:, :, lo:hi])
            return banks[g][h][:, at : at + hi - lo], (lambda t: t[g][:, k, lo:hi])

        def square(g, k, lo, hi, h, at):
            src, pick = views(g, k, lo, hi, h, at)
            nc.scalar.activation(out=pick(sq), in_=src, func=ACT.Square)

        def keep(g, k, lo, hi, h, at):
            src, pick = views(g, k, lo, hi, h, at)
            nc.vector.tensor_copy(out=pick(kept), in_=src)

        def times(g, k, lo, hi, h, at):
            src, pick = views(g, k, lo, hi, h, at)
            nc.vector.tensor_tensor(out=pick(sq), in0=src, in1=pick(kept), op=ALU.mult)

        def add(g, lo, hi):
            nc.vector.scalar_tensor_tensor(
                out=tot[g][:, lo:hi], in0=sq[g][:, 0, lo:hi], scalar=EPS, in1=sq[g][:, 1, lo:hi], op0=ALU.add, op1=ALU.add
            )

        def regroup(g, lo, hi, eng=nc.sync):
            eng.dma_start(out=power[R * g : R * g + R, :, lo:hi], in_=tot[g][:, lo:hi])

        def log(lo, hi):
            nc.scalar.activation(out=logs[:, :, lo:hi], in_=power[:, :, lo:hi], func=ACT.Ln)

        def halve_v(lo, hi):
            nc.vector.tensor_scalar(out=y[:, :, lo:hi], in0=logs[:, :, lo:hi], scalar1=0.5, scalar2=None, op0=ALU.mult)

        def halve_a(lo, hi):
            nc.scalar.activation(out=y[:, :, lo:hi], in_=logs[:, :, lo:hi], func=ACT.Copy, scale=0.5)

        def round_y(lo, hi):
            nc.vector.tensor_scalar(
                out=walk_dst(y_bf[:, PACK * lo : PACK * hi]),
                in0=walk_src(logs[:, :, lo:hi]),
                scalar1=0.5,
                scalar2=None,
                op0=ALU.mult,
            )

        def quant_y(lo, hi):
            nc.vector.quantize_mx(
                out=y_codes[:, lo:hi].bitcast(FP8X4), scales=y_scales[:, lo:hi], in_=y_bf[:, PACK * lo : PACK * hi]
            )

        def store_y(lo, hi, eng):
            eng.dma_start(out=y_rows[:, :, lo:hi], in_=y[:, :, lo:hi])

        def store_words(lo, hi, eng):
            eng.dma_start(out=words_out[:, lo:hi], in_=y_codes[:, lo:hi].bitcast(I32))

        def store_scales(engs):
            for q in range(4):
                engs[q].dma_start(out=scales_out[4 * q : 4 * q + 4, :], in_=y_scales[R * q : R * q + 4, :].bitcast(I32))

        V, A, S = nc.vector.tensor_copy, nc.scalar.copy, nc.sync
        Q = nc.scalar
        load_f()
        load_x(0)
        load_x(1)
        load_x(2)
        nc.vector.memset(one[:], 1.0)
        nc.scalar.activation(out=warm[:], in_=one[:], func=ACT.Ln)
        nc.vector.memset(f_q[0][:, M:], 0)
        round_f(V)
        quant_f()
        round_x(0, 128, V)
        round_x(208, 256, A)
        quant_x(0, 128)
        round_x(128, 208, V)
        for g in ORDER:
            product(g, 0, 0, 0, 0)
        quant_x(128, 256)
        round_x(256, 512, V)
        quant_x(256, 512)
        for g in ORDER:
            square(g, 0, 0, 128, 0, 0)
        for g in ORDER:
            product(g, 0, 1, 1, 0)
        for g in ORDER:
            square(g, 0, 128, 256, 1, 0)
        for c in range(2):
            for g in ORDER:
                product(g, 1, c, 0, 1 + c)
        for g in ORDER:
            for k in range(2):
                product(g, k, 2, 1, k)
        for g in ORDER:
            square(g, 1, 0, 128, 0, CH)
            add(g, 0, 128)
            regroup(g, 0, 128)
        for g in ORDER:
            square(g, 1, 128, 256, 0, 256)
            add(g, 128, 256)
            regroup(g, 128, 256)
        for g in ORDER:
            for k in range(2):
                product(g, k, 3, 0, k)
        for g in ORDER:
            square(g, None, 256, 384, 1, 0)
            add(g, 256, 384)
            regroup(g, 256, 384)
        for g in ORDER:
            square(g, None, 384, 512, 0, 0)
            add(g, 384, 512)
            regroup(g, 384, 512)
        log(0, 128)
        halve_v(0, 128)
        store_y(0, 128, S)
        round_y(0, 128)
        log(128, 256)
        halve_v(128, 256)
        store_y(128, 256, S)
        quant_y(0, 128)
        round_y(128, 256)
        log(256, 384)
        halve_v(256, 384)
        store_y(256, 384, S)
        quant_y(128, 256)
        round_y(256, 384)
        store_words(0, 256, S)
        quant_y(256, 384)
        log(384, 512)
        round_y(384, 512)
        halve_a(384, 512)
        store_y(384, 512, Q)
        quant_y(384, 512)
        store_words(256, 512, S)
        store_scales((S, Q, S, Q))
